import numpy as np
import ml_dtypes

BF16 = ml_dtypes.bfloat16


def bf(x):
    return np.asarray(x, np.float32).astype(BF16)


def f32(x):
    return np.asarray(x, np.float32)


def f64(x):
    return np.asarray(x).astype(np.float64)


def striped(idx):
    return np.tile(idx.reshape(-1, 16).T, (8, 1))


S, K, M, N, E, Q = 256, 256, 128, 256, 2, 128


def setup_inputs():
    return {"table": bf(np.random.standard_normal((K, S))), "w": bf(np.random.standard_normal((E, K, M)) / np.sqrt(K)), "c": f32(0.2 + 0.8 * np.random.random_sample((1, N))), "offs": striped(np.sort(np.random.permutation(S).reshape(E, Q), axis=1).reshape(-1))}


def reference(table, w, c, offs):
    idx = offs[:16].T.reshape(-1)
    x = f64(table)[:, idx]
    y = np.concatenate([f64(w)[e].T @ x[:, e * Q : (e + 1) * Q] for e in range(E)], axis=1)
    return y * f64(c)

@@ -1,0 +1,61 @@
+import concourse.mybir as mybir
+
+BF16, F32, U16 = mybir.dt.bfloat16, mybir.dt.float32, mybir.dt.uint16
+
+P = 128
+S = 256
+K = 256
+M = 128
+N = 256
+E = 2
+Q = N // E
+KB = K // P
+PER_COLUMN = 16
+
+FLOPS = 2 * K * M * N
+
+
+def tile_gather_matmul_kernel(tc, table, w, c, offs, out):
+    nc = tc.nc
+    with (
+        tc.tile_pool(name="held", bufs=1) as held,
+        tc.psum_pool(name="psum", bufs=1) as psum,
+    ):
+        offsets = held.tile([P, N // PER_COLUMN], U16, name="offsets")
+        nc.sync.dma_start(offsets[:], offs)
+
+        windows = []
+        for b in range(KB):
+            window = held.tile([P, S], BF16, name="window%d" % b)
+            nc.sync.dma_start(window[:], table[b * P : (b + 1) * P, :])
+            windows.append(window)
+
+        c_row = held.tile([1, N], F32, name="c_row")
+        nc.scalar.dma_start(c_row[:], c)
+
+        weights = held.tile([P, E * KB, M], BF16, name="weights")
+        nc.scalar.dma_start(weights[:], w.rearrange("e (b p) m -> p (e b) m", p=P))
+
+        ones = held.tile([1, P], F32, name="ones")
+        nc.vector.memset(ones[:], 1.0)
+        spread = psum.tile([P, N], F32, name="spread")
+        nc.tensor.matmul(spread[:], ones[:], c_row[:], start=True, stop=True)
+        factor = held.tile([P, N], F32, name="factor")
+        nc.vector.tensor_copy(factor[:], spread[:])
+
+        result = held.tile([P, N], F32, name="result")
+        store_queues = [nc.scalar, nc.sync]
+        for e in range(E):
+            piece = offsets[:, e * Q // PER_COLUMN : (e + 1) * Q // PER_COLUMN]
+            columns = slice(e * Q, (e + 1) * Q)
+            bank = psum.tile([P, Q], F32, name="bank%d" % e)
+            for b in range(KB):
+                nc.tensor.matmul(
+                    bank[:],
+                    weights[:, e * KB + b, :],
+                    windows[b][:].indirect(piece),
+                    start=(b == 0),
+                    stop=(b == KB - 1),
+                )
+            nc.vector.tensor_tensor(result[:, columns], bank[:], factor[:, columns], mybir.AluOpType.mult)
+            store_queues[e].dma_start(out[:, columns], result[:, columns])

@@ -24,17 +24,18 @@ def tile_gather_matmul_kernel(tc, table, w, c, offs, out):
         offsets = held.tile([P, N // PER_COLUMN], U16, name="offsets")
         nc.sync.dma_start(offsets[:], offs)
 
+        table_blocks = table.rearrange("(p b) s -> p b s", b=KB)
         windows = []
         for b in range(KB):
             window = held.tile([P, S], BF16, name="window%d" % b)
-            nc.sync.dma_start(window[:], table[b * P : (b + 1) * P, :])
+            nc.sync.dma_start(window[:], table_blocks[:, b, :])
             windows.append(window)
 
         c_row = held.tile([1, N], F32, name="c_row")
         nc.scalar.dma_start(c_row[:], c)
 
-        weights = held.tile([P, E * KB, M], BF16, name="weights")
-        nc.scalar.dma_start(weights[:], w.rearrange("e (b p) m -> p (e b) m", p=P))
+        weights = held.tile([P, E, KB * M], BF16, name="weights")
+        nc.scalar.dma_start(weights[:], w.rearrange("e (p b) m -> p e (b m)", b=KB))
 
         ones = held.tile([1, P], F32, name="ones")
         nc.vector.memset(ones[:], 1.0)
@@ -52,7 +53,7 @@ def tile_gather_matmul_kernel(tc, table, w, c, offs, out):
             for b in range(KB):
                 nc.tensor.matmul(
                     bank[:],
-                    weights[:, e * KB + b, :],
+                    weights[:, e, b * M : (b + 1) * M],
                     windows[b][:].indirect(piece),
                     start=(b == 0),
                     stop=(b == KB - 1),

@@ -21,6 +21,10 @@ def tile_gather_matmul_kernel(tc, table, w, c, offs, out):
         tc.tile_pool(name="held", bufs=1) as held,
         tc.psum_pool(name="psum", bufs=1) as psum,
     ):
+
+        c_row = held.tile([1, N], F32, name="c_row")
+        nc.sync.dma_start(c_row[:], c)
+
         offsets = held.tile([P, N // PER_COLUMN], U16, name="offsets")
         nc.sync.dma_start(offsets[:], offs)
 
@@ -31,11 +35,8 @@ def tile_gather_matmul_kernel(tc, table, w, c, offs, out):
             nc.sync.dma_start(window[:], table_blocks[:, b, :])
             windows.append(window)
 
-        c_row = held.tile([1, N], F32, name="c_row")
-        nc.scalar.dma_start(c_row[:], c)
-
         weights = held.tile([P, E, KB * M], BF16, name="weights")
-        nc.scalar.dma_start(weights[:], w.rearrange("e (p b) m -> p e (b m)", b=KB))
+        nc.sync.dma_start(weights[:], w.rearrange("e (p b) m -> p e (b m)", b=KB))
 
         ones = held.tile([1, P], F32, name="ones")
         nc.vector.memset(ones[:], 1.0)
@@ -45,7 +46,6 @@ def tile_gather_matmul_kernel(tc, table, w, c, offs, out):
         nc.vector.tensor_copy(factor[:], spread[:])
 
         result = held.tile([P, N], F32, name="result")
-        store_queues = [nc.scalar, nc.sync]
         for e in range(E):
             piece = offsets[:, e * Q // PER_COLUMN : (e + 1) * Q // PER_COLUMN]
             columns = slice(e * Q, (e + 1) * Q)
@@ -59,4 +59,4 @@ def tile_gather_matmul_kernel(tc, table, w, c, offs, out):
                     stop=(b == KB - 1),
                 )
             nc.vector.tensor_tensor(result[:, columns], bank[:], factor[:, columns], mybir.AluOpType.mult)
-            store_queues[e].dma_start(out[:, columns], result[:, columns])
+            nc.sync.dma_start(out[:, columns], result[:, columns])

@@ -40,10 +40,13 @@ def tile_gather_matmul_kernel(tc, table, w, c, offs, out):
 
         ones = held.tile([1, P], F32, name="ones")
         nc.vector.memset(ones[:], 1.0)
-        spread = psum.tile([P, N], F32, name="spread")
-        nc.tensor.matmul(spread[:], ones[:], c_row[:], start=True, stop=True)
-        factor = held.tile([P, N], F32, name="factor")
-        nc.vector.tensor_copy(factor[:], spread[:])
+        factors = []
+        for e in range(E):
+            spread = psum.tile([P, Q], F32, name="spread%d" % e)
+            nc.tensor.matmul(spread[:], ones[:], c_row[:, e * Q : (e + 1) * Q], start=True, stop=True)
+            factor = held.tile([P, Q], F32, name="factor%d" % e)
+            nc.vector.tensor_copy(factor[:], spread[:])
+            factors.append(factor)
 
         result = held.tile([P, N], F32, name="result")
         for e in range(E):
@@ -58,5 +61,5 @@ def tile_gather_matmul_kernel(tc, table, w, c, offs, out):
                     start=(b == 0),
                     stop=(b == KB - 1),
                 )
-            nc.vector.tensor_tensor(result[:, columns], bank[:], factor[:, columns], mybir.AluOpType.mult)
+            nc.vector.tensor_tensor(result[:, columns], bank[:], factors[e][:], mybir.AluOpType.mult)
             nc.sync.dma_start(out[:, columns], result[:, columns])

@@ -38,6 +38,11 @@ def tile_gather_matmul_kernel(tc, table, w, c, offs, out):
         weights = held.tile([P, E, KB * M], BF16, name="weights")
         nc.sync.dma_start(weights[:], w.rearrange("e (p b) m -> p e (b m)", b=KB))
 
+        zero = held.tile([P, 1], BF16, name="zero")
+        nc.vector.memset(zero[:], 0.0)
+        unread = psum.tile([P, Q], F32, name="unread")
+        nc.tensor.matmul(unread[:], zero[:].to_broadcast([P, P]), zero[:].to_broadcast([P, Q]), start=True, stop=True)
+
         ones = held.tile([1, P], F32, name="ones")
         nc.vector.memset(ones[:], 1.0)
         factors = []

@@ -11,6 +11,9 @@ E = 2
 Q = N // E
 KB = K // P
 PER_COLUMN = 16
+SQUARE = 32
+CHUNKS = N // SQUARE
+TURNED = 64
 
 FLOPS = 2 * K * M * N
 
@@ -22,8 +25,9 @@ def tile_gather_matmul_kernel(tc, table, w, c, offs, out):
         tc.psum_pool(name="psum", bufs=1) as psum,
     ):
 
-        c_row = held.tile([1, N], F32, name="c_row")
-        nc.sync.dma_start(c_row[:], c)
+        chunks = held.tile([P, SQUARE], F32, name="chunks", align_bytes=TURNED)
+        c_chunks = c.rearrange("o (r i) -> (o r) i", i=SQUARE)
+        nc.sync.dma_start(chunks[:], c_chunks.unsqueeze(0).to_broadcast([P // CHUNKS, CHUNKS, SQUARE]))
 
         offsets = held.tile([P, N // PER_COLUMN], U16, name="offsets")
         nc.sync.dma_start(offsets[:], offs)
@@ -38,25 +42,20 @@ def tile_gather_matmul_kernel(tc, table, w, c, offs, out):
         weights = held.tile([P, E, KB * M], BF16, name="weights")
         nc.sync.dma_start(weights[:], w.rearrange("e (p b) m -> p e (b m)", b=KB))
 
-        zero = held.tile([P, 1], BF16, name="zero")
-        nc.vector.memset(zero[:], 0.0)
-        unread = psum.tile([P, Q], F32, name="unread")
-        nc.tensor.matmul(unread[:], zero[:].to_broadcast([P, P]), zero[:].to_broadcast([P, Q]), start=True, stop=True)
-
-        ones = held.tile([1, P], F32, name="ones")
-        nc.vector.memset(ones[:], 1.0)
-        factors = []
+        columns = held.tile([P, SQUARE], F32, name="columns", align_bytes=TURNED)
+        nc.vector.transpose(columns[:], chunks[:])
+        repeated = held.tile([P, CHUNKS, SQUARE], F32, name="repeated", align_bytes=TURNED)
+        nc.vector.tensor_copy(repeated[:], columns[:, 0:CHUNKS].unsqueeze(2).to_broadcast([P, CHUNKS, SQUARE]))
+        repeated_flat = repeated[:].rearrange("p b i -> p (b i)")
+        factor = held.tile([P, N], F32, name="factor", align_bytes=TURNED)
         for e in range(E):
-            spread = psum.tile([P, Q], F32, name="spread%d" % e)
-            nc.tensor.matmul(spread[:], ones[:], c_row[:, e * Q : (e + 1) * Q], start=True, stop=True)
-            factor = held.tile([P, Q], F32, name="factor%d" % e)
-            nc.vector.tensor_copy(factor[:], spread[:])
-            factors.append(factor)
+            entries = slice(e * Q, (e + 1) * Q)
+            nc.vector.transpose(factor[:, entries], repeated_flat[:, entries])
 
         result = held.tile([P, N], F32, name="result")
         for e in range(E):
             piece = offsets[:, e * Q // PER_COLUMN : (e + 1) * Q // PER_COLUMN]
-            columns = slice(e * Q, (e + 1) * Q)
+            entries = slice(e * Q, (e + 1) * Q)
             bank = psum.tile([P, Q], F32, name="bank%d" % e)
             for b in range(KB):
                 nc.tensor.matmul(
@@ -66,5 +65,5 @@ def tile_gather_matmul_kernel(tc, table, w, c, offs, out):
                     start=(b == 0),
                     stop=(b == KB - 1),
                 )
-            nc.vector.tensor_tensor(result[:, columns], bank[:], factors[e][:], mybir.AluOpType.mult)
-            nc.sync.dma_start(out[:, columns], result[:, columns])
+            nc.vector.tensor_tensor(result[:, entries], bank[:], factor[:, entries], mybir.AluOpType.mult)
+            nc.sync.dma_start(out[:, entries], result[:, entries])

@@ -14,6 +14,8 @@ PER_COLUMN = 16
 SQUARE = 32
 CHUNKS = N // SQUARE
 TURNED = 64
+BANK = 512
+WARM_UPS = 4
 
 FLOPS = 2 * K * M * N
 
@@ -41,6 +43,12 @@ def tile_gather_matmul_kernel(tc, table, w, c, offs, out):
 
         weights = held.tile([P, E, KB * M], BF16, name="weights")
         nc.sync.dma_start(weights[:], w.rearrange("e (p b) m -> p e (b m)", b=KB))
+
+        zero = held.tile([P, 1], BF16, name="zero")
+        nc.vector.memset(zero[:], 0.0)
+        unread = psum.tile([P, BANK], F32, name="unread")
+        for warm_up in range(WARM_UPS):
+            nc.tensor.matmul(unread[:], zero[:].to_broadcast([P, P]), zero[:].to_broadcast([P, BANK]), start=True, stop=True)
 
         columns = held.tile([P, SQUARE], F32, name="columns", align_bytes=TURNED)
         nc.vector.transpose(columns[:], chunks[:])

@@ -54,11 +54,8 @@ def tile_gather_matmul_kernel(tc, table, w, c, offs, out):
         nc.vector.transpose(columns[:], chunks[:])
         repeated = held.tile([P, CHUNKS, SQUARE], F32, name="repeated", align_bytes=TURNED)
         nc.vector.tensor_copy(repeated[:], columns[:, 0:CHUNKS].unsqueeze(2).to_broadcast([P, CHUNKS, SQUARE]))
-        repeated_flat = repeated[:].rearrange("p b i -> p (b i)")
         factor = held.tile([P, N], F32, name="factor", align_bytes=TURNED)
-        for e in range(E):
-            entries = slice(e * Q, (e + 1) * Q)
-            nc.vector.transpose(factor[:, entries], repeated_flat[:, entries])
+        nc.vector.transpose(factor[:], repeated[:].rearrange("p b i -> p (b i)"))
 
         result = held.tile([P, N], F32, name="result")
         for e in range(E):

@@ -14,8 +14,6 @@ PER_COLUMN = 16
 SQUARE = 32
 CHUNKS = N // SQUARE
 TURNED = 64
-BANK = 512
-WARM_UPS = 4
 
 FLOPS = 2 * K * M * N
 
@@ -34,21 +32,15 @@ def tile_gather_matmul_kernel(tc, table, w, c, offs, out):
         offsets = held.tile([P, N // PER_COLUMN], U16, name="offsets")
         nc.sync.dma_start(offsets[:], offs)
 
+        weights = held.tile([P, E, KB * M], BF16, name="weights")
+        nc.sync.dma_start(weights[:], w.rearrange("e (p b) m -> p e (b m)", b=KB))
+
         table_blocks = table.rearrange("(p b) s -> p b s", b=KB)
         windows = []
         for b in range(KB):
             window = held.tile([P, S], BF16, name="window%d" % b)
             nc.sync.dma_start(window[:], table_blocks[:, b, :])
             windows.append(window)
-
-        weights = held.tile([P, E, KB * M], BF16, name="weights")
-        nc.sync.dma_start(weights[:], w.rearrange("e (p b) m -> p e (b m)", b=KB))
-
-        zero = held.tile([P, 1], BF16, name="zero")
-        nc.vector.memset(zero[:], 0.0)
-        unread = psum.tile([P, BANK], F32, name="unread")
-        for warm_up in range(WARM_UPS):
-            nc.tensor.matmul(unread[:], zero[:].to_broadcast([P, P]), zero[:].to_broadcast([P, BANK]), start=True, stop=True)
 
         columns = held.tile([P, SQUARE], F32, name="columns", align_bytes=TURNED)
         nc.vector.transpose(columns[:], chunks[:])
@@ -57,18 +49,20 @@ def tile_gather_matmul_kernel(tc, table, w, c, offs, out):
         factor = held.tile([P, N], F32, name="factor", align_bytes=TURNED)
         nc.vector.transpose(factor[:], repeated[:].rearrange("p b i -> p (b i)"))
 
-        result = held.tile([P, N], F32, name="result")
-        for e in range(E):
-            piece = offsets[:, e * Q // PER_COLUMN : (e + 1) * Q // PER_COLUMN]
-            entries = slice(e * Q, (e + 1) * Q)
-            bank = psum.tile([P, Q], F32, name="bank%d" % e)
-            for b in range(KB):
+        pieces = [offsets[:, e * Q // PER_COLUMN : (e + 1) * Q // PER_COLUMN] for e in range(E)]
+        banks = [psum.tile([P, Q], F32, name="bank%d" % e) for e in range(E)]
+        for b in range(KB):
+            for e in range(E):
                 nc.tensor.matmul(
-                    bank[:],
+                    banks[e][:],
                     weights[:, e, b * M : (b + 1) * M],
-                    windows[b][:].indirect(piece),
+                    windows[b][:].indirect(pieces[e]),
                     start=(b == 0),
                     stop=(b == KB - 1),
                 )
-            nc.vector.tensor_tensor(result[:, entries], bank[:], factor[:, entries], mybir.AluOpType.mult)
+
+        result = held.tile([P, N], F32, name="result")
+        for e in range(E):
+            entries = slice(e * Q, (e + 1) * Q)
+            nc.vector.tensor_tensor(result[:, entries], banks[e][:], factor[:, entries], mybir.AluOpType.mult)
             nc.sync.dma_start(out[:, entries], result[:, entries])

@@ -32,15 +32,14 @@ def tile_gather_matmul_kernel(tc, table, w, c, offs, out):
         offsets = held.tile([P, N // PER_COLUMN], U16, name="offsets")
         nc.sync.dma_start(offsets[:], offs)
 
-        weights = held.tile([P, E, KB * M], BF16, name="weights")
-        nc.sync.dma_start(weights[:], w.rearrange("e (p b) m -> p e (b m)", b=KB))
-
+        expert_weights = w.rearrange("e (p b) m -> e p (b m)", b=KB)
         table_blocks = table.rearrange("(p b) s -> p b s", b=KB)
-        windows = []
+        weights = [held.tile([P, KB * M], BF16, name="weights%d" % e) for e in range(E)]
+        windows = [held.tile([P, S], BF16, name="window%d" % b) for b in range(KB)]
+        nc.sync.dma_start(weights[0][:], expert_weights[0])
         for b in range(KB):
-            window = held.tile([P, S], BF16, name="window%d" % b)
-            nc.sync.dma_start(window[:], table_blocks[:, b, :])
-            windows.append(window)
+            nc.sync.dma_start(windows[b][:], table_blocks[:, b, :])
+        nc.sync.dma_start(weights[1][:], expert_weights[1])
 
         columns = held.tile([P, SQUARE], F32, name="columns", align_bytes=TURNED)
         nc.vector.transpose(columns[:], chunks[:])
@@ -49,20 +48,18 @@ def tile_gather_matmul_kernel(tc, table, w, c, offs, out):
         factor = held.tile([P, N], F32, name="factor", align_bytes=TURNED)
         nc.vector.transpose(factor[:], repeated[:].rearrange("p b i -> p (b i)"))
 
-        pieces = [offsets[:, e * Q // PER_COLUMN : (e + 1) * Q // PER_COLUMN] for e in range(E)]
-        banks = [psum.tile([P, Q], F32, name="bank%d" % e) for e in range(E)]
-        for b in range(KB):
-            for e in range(E):
+        result = held.tile([P, N], F32, name="result")
+        for e in range(E):
+            piece = offsets[:, e * Q // PER_COLUMN : (e + 1) * Q // PER_COLUMN]
+            entries = slice(e * Q, (e + 1) * Q)
+            bank = psum.tile([P, Q], F32, name="bank%d" % e)
+            for b in range(KB):
                 nc.tensor.matmul(
-                    banks[e][:],
-                    weights[:, e, b * M : (b + 1) * M],
-                    windows[b][:].indirect(pieces[e]),
+                    bank[:],
+                    weights[e][:, b * M : (b + 1) * M],
+                    windows[b][:].indirect(piece),
                     start=(b == 0),
                     stop=(b == KB - 1),
                 )
-
-        result = held.tile([P, N], F32, name="result")
-        for e in range(E):
-            entries = slice(e * Q, (e + 1) * Q)
-            nc.vector.tensor_tensor(result[:, entries], banks[e][:], factor[:, entries], mybir.AluOpType.mult)
+            nc.vector.tensor_tensor(result[:, entries], bank[:], factor[:, entries], mybir.AluOpType.mult)
             nc.sync.dma_start(out[:, entries], result[:, entries])

@@ -14,6 +14,8 @@ PER_COLUMN = 16
 SQUARE = 32
 CHUNKS = N // SQUARE
 TURNED = 64
+BANK = 512
+WARM_UPS = 3
 
 FLOPS = 2 * K * M * N
 
@@ -40,6 +42,12 @@ def tile_gather_matmul_kernel(tc, table, w, c, offs, out):
         for b in range(KB):
             nc.sync.dma_start(windows[b][:], table_blocks[:, b, :])
         nc.sync.dma_start(weights[1][:], expert_weights[1])
+
+        zero = held.tile([P, 1], BF16, name="zero")
+        nc.vector.memset(zero[:], 0.0)
+        unread = psum.tile([P, BANK], F32, name="unread")
+        for warm_up in range(WARM_UPS):
+            nc.tensor.matmul(unread[:], zero[:].to_broadcast([P, P]), zero[:].to_broadcast([P, BANK]), start=True, stop=True)
 
         columns = held.tile([P, SQUARE], F32, name="columns", align_bytes=TURNED)
         nc.vector.transpose(columns[:], chunks[:])

@@ -49,6 +49,15 @@ def tile_gather_matmul_kernel(tc, table, w, c, offs, out):
         for warm_up in range(WARM_UPS):
             nc.tensor.matmul(unread[:], zero[:].to_broadcast([P, P]), zero[:].to_broadcast([P, BANK]), start=True, stop=True)
 
+        idle = held.tile([P, SQUARE], F32, name="idle", align_bytes=TURNED)
+        nc.vector.memset(idle[:], 0.0)
+        idle_turned = held.tile([P, SQUARE], F32, name="idle_turned", align_bytes=TURNED)
+        nc.vector.transpose(idle_turned[:], idle[:])
+        idle_repeated = held.tile([P, CHUNKS, SQUARE], F32, name="idle_repeated")
+        nc.vector.tensor_copy(idle_repeated[:], idle_turned[:, 0:CHUNKS].unsqueeze(2).to_broadcast([P, CHUNKS, SQUARE]))
+        idle_product = held.tile([P, SQUARE], F32, name="idle_product")
+        nc.vector.tensor_tensor(idle_product[:], idle[:], idle_turned[:], mybir.AluOpType.mult)
+
         columns = held.tile([P, SQUARE], F32, name="columns", align_bytes=TURNED)
         nc.vector.transpose(columns[:], chunks[:])
         repeated = held.tile([P, CHUNKS, SQUARE], F32, name="repeated", align_bytes=TURNED)

@@ -14,8 +14,8 @@ PER_COLUMN = 16
 SQUARE = 32
 CHUNKS = N // SQUARE
 TURNED = 64
-BANK = 512
-WARM_UPS = 3
+WARM_COLUMNS = 256
+WARM_UPS = 7
 
 FLOPS = 2 * K * M * N
 
@@ -45,9 +45,9 @@ def tile_gather_matmul_kernel(tc, table, w, c, offs, out):
 
         zero = held.tile([P, 1], BF16, name="zero")
         nc.vector.memset(zero[:], 0.0)
-        unread = psum.tile([P, BANK], F32, name="unread")
+        unread = psum.tile([P, WARM_COLUMNS], F32, name="unread")
         for warm_up in range(WARM_UPS):
-            nc.tensor.matmul(unread[:], zero[:].to_broadcast([P, P]), zero[:].to_broadcast([P, BANK]), start=True, stop=True)
+            nc.tensor.matmul(unread[:], zero[:].to_broadcast([P, P]), zero[:].to_broadcast([P, WARM_COLUMNS]), start=True, stop=True)
 
         idle = held.tile([P, SQUARE], F32, name="idle", align_bytes=TURNED)
         nc.vector.memset(idle[:], 0.0)

@@ -61,9 +61,13 @@ def tile_gather_matmul_kernel(tc, table, w, c, offs, out):
         columns = held.tile([P, SQUARE], F32, name="columns", align_bytes=TURNED)
         nc.vector.transpose(columns[:], chunks[:])
         repeated = held.tile([P, CHUNKS, SQUARE], F32, name="repeated", align_bytes=TURNED)
-        nc.vector.tensor_copy(repeated[:], columns[:, 0:CHUNKS].unsqueeze(2).to_broadcast([P, CHUNKS, SQUARE]))
         factor = held.tile([P, N], F32, name="factor", align_bytes=TURNED)
-        nc.vector.transpose(factor[:], repeated[:].rearrange("p b i -> p (b i)"))
+        for e in range(E):
+            own = slice(e * CHUNKS // E, (e + 1) * CHUNKS // E)
+            nc.vector.tensor_copy(repeated[:, own, :], columns[:, own].unsqueeze(2).to_broadcast([P, CHUNKS // E, SQUARE]))
+        for e in range(E):
+            own = slice(e * CHUNKS // E, (e + 1) * CHUNKS // E)
+            nc.vector.transpose(factor[:, e * Q : (e + 1) * Q], repeated[:, own, :].rearrange("p b i -> p (b i)"))
 
         result = held.tile([P, N], F32, name="result")
         for e in range(E):

@@ -14,6 +14,7 @@ PER_COLUMN = 16
 SQUARE = 32
 CHUNKS = N // SQUARE
 TURNED = 64
+RUN = 512
 WARM_COLUMNS = 256
 WARM_UPS = 7
 
@@ -36,8 +37,8 @@ def tile_gather_matmul_kernel(tc, table, w, c, offs, out):
 
         expert_weights = w.rearrange("e (p b) m -> e p (b m)", b=KB)
         table_blocks = table.rearrange("(p b) s -> p b s", b=KB)
-        weights = [held.tile([P, KB * M], BF16, name="weights%d" % e) for e in range(E)]
-        windows = [held.tile([P, S], BF16, name="window%d" % b) for b in range(KB)]
+        weights = [held.tile([P, KB * M], BF16, name="weights%d" % e, align_bytes=RUN) for e in range(E)]
+        windows = [held.tile([P, S], BF16, name="window%d" % b, align_bytes=RUN) for b in range(KB)]
         nc.sync.dma_start(weights[0][:], expert_weights[0])
         for b in range(KB):
             nc.sync.dma_start(windows[b][:], table_blocks[:, b, :])
@@ -69,7 +70,7 @@ def tile_gather_matmul_kernel(tc, table, w, c, offs, out):
             own = slice(e * CHUNKS // E, (e + 1) * CHUNKS // E)
             nc.vector.transpose(factor[:, e * Q : (e + 1) * Q], repeated[:, own, :].rearrange("p b i -> p (b i)"))
 
-        result = held.tile([P, N], F32, name="result")
+        result = held.tile([P, N], F32, name="result", align_bytes=RUN)
         for e in range(E):
             piece = offsets[:, e * Q // PER_COLUMN : (e + 1) * Q // PER_COLUMN]
             entries = slice(e * Q, (e + 1) * Q)

@@ -15,6 +15,7 @@ SQUARE = 32
 CHUNKS = N // SQUARE
 TURNED = 64
 RUN = 512
+BLOCK = 256
 WARM_COLUMNS = 256
 WARM_UPS = 7
 
@@ -28,11 +29,11 @@ def tile_gather_matmul_kernel(tc, table, w, c, offs, out):
         tc.psum_pool(name="psum", bufs=1) as psum,
     ):
 
-        chunks = held.tile([P, SQUARE], F32, name="chunks", align_bytes=TURNED)
+        chunks = held.tile([P, SQUARE], F32, name="chunks", align_bytes=BLOCK)
         c_chunks = c.rearrange("o (r i) -> (o r) i", i=SQUARE)
         nc.sync.dma_start(chunks[:], c_chunks.unsqueeze(0).to_broadcast([P // CHUNKS, CHUNKS, SQUARE]))
 
-        offsets = held.tile([P, N // PER_COLUMN], U16, name="offsets")
+        offsets = held.tile([P, N // PER_COLUMN], U16, name="offsets", align_bytes=BLOCK)
         nc.sync.dma_start(offsets[:], offs)
 
         expert_weights = w.rearrange("e (p b) m -> e p (b m)", b=KB)

@@ -16,8 +16,8 @@ CHUNKS = N // SQUARE
 TURNED = 64
 RUN = 512
 BLOCK = 256
-WARM_COLUMNS = 256
-WARM_UPS = 7
+WARM_COLUMNS = 512
+WARM_UPS = 3
 
 FLOPS = 2 * K * M * N
 

@@ -60,10 +60,10 @@ def tile_gather_matmul_kernel(tc, table, w, c, offs, out):
         idle_product = held.tile([P, SQUARE], F32, name="idle_product")
         nc.vector.tensor_tensor(idle_product[:], idle[:], idle_turned[:], mybir.AluOpType.mult)
 
-        columns = held.tile([P, SQUARE], F32, name="columns", align_bytes=TURNED)
+        columns = held.tile([P, SQUARE], F32, name="columns", align_bytes=BLOCK)
         nc.vector.transpose(columns[:], chunks[:])
-        repeated = held.tile([P, CHUNKS, SQUARE], F32, name="repeated", align_bytes=TURNED)
-        factor = held.tile([P, N], F32, name="factor", align_bytes=TURNED)
+        repeated = held.tile([P, CHUNKS, SQUARE], F32, name="repeated", align_bytes=RUN)
+        factor = held.tile([P, N], F32, name="factor", align_bytes=RUN)
         for e in range(E):
             own = slice(e * CHUNKS // E, (e + 1) * CHUNKS // E)
             nc.vector.tensor_copy(repeated[:, own, :], columns[:, own].unsqueeze(2).to_broadcast([P, CHUNKS // E, SQUARE]))

@@ -17,6 +17,7 @@ TURNED = 64
 RUN = 512
 BLOCK = 256
 WARM_COLUMNS = 512
+BUSY_STEPS = 4
 WARM_UPS = 3
 
 FLOPS = 2 * K * M * N
@@ -86,3 +87,8 @@ def tile_gather_matmul_kernel(tc, table, w, c, offs, out):
                 )
             nc.vector.tensor_tensor(result[:, entries], bank[:], factor[:, entries], mybir.AluOpType.mult)
             nc.sync.dma_start(out[:, entries], result[:, entries])
+
+        kept_busy = [held.tile([P, SQUARE], F32, name="kept_busy%d" % step) for step in range(BUSY_STEPS)]
+        nc.vector.tensor_copy(kept_busy[0][:], result[:, N - SQUARE : N])
+        for step in range(1, BUSY_STEPS):
+            nc.vector.tensor_copy(kept_busy[step][:], kept_busy[step - 1][:])

import concourse.mybir as mybir

BF16, F32, U16 = mybir.dt.bfloat16, mybir.dt.float32, mybir.dt.uint16

P = 128
S = 256
K = 256
M = 128
N = 256
E = 2
Q = N // E
KB = K // P
PER_COLUMN = 16
SQUARE = 32
CHUNKS = N // SQUARE
TURNED = 64
RUN = 512
BLOCK = 256
WARM_COLUMNS = 512
BUSY_STEPS = 4
WARM_UPS = 3

FLOPS = 2 * K * M * N


def tile_gather_matmul_kernel(tc, table, w, c, offs, out):
    nc = tc.nc
    with (
        tc.tile_pool(name="held", bufs=1) as held,
        tc.psum_pool(name="psum", bufs=1) as psum,
    ):

        chunks = held.tile([P, SQUARE], F32, name="chunks", align_bytes=BLOCK)
        c_chunks = c.rearrange("o (r i) -> (o r) i", i=SQUARE)
        nc.sync.dma_start(chunks[:], c_chunks.unsqueeze(0).to_broadcast([P // CHUNKS, CHUNKS, SQUARE]))

        offsets = held.tile([P, N // PER_COLUMN], U16, name="offsets", align_bytes=BLOCK)
        nc.sync.dma_start(offsets[:], offs)

        expert_weights = w.rearrange("e (p b) m -> e p (b m)", b=KB)
        table_blocks = table.rearrange("(p b) s -> p b s", b=KB)
        weights = [held.tile([P, KB * M], BF16, name="weights%d" % e, align_bytes=RUN) for e in range(E)]
        windows = [held.tile([P, S], BF16, name="window%d" % b, align_bytes=RUN) for b in range(KB)]
        nc.sync.dma_start(weights[0][:], expert_weights[0])
        for b in range(KB):
            nc.sync.dma_start(windows[b][:], table_blocks[:, b, :])
        nc.sync.dma_start(weights[1][:], expert_weights[1])

        zero = held.tile([P, 1], BF16, name="zero")
        nc.vector.memset(zero[:], 0.0)
        unread = psum.tile([P, WARM_COLUMNS], F32, name="unread")
        for warm_up in range(WARM_UPS):
            nc.tensor.matmul(unread[:], zero[:].to_broadcast([P, P]), zero[:].to_broadcast([P, WARM_COLUMNS]), start=True, stop=True)

        idle = held.tile([P, SQUARE], F32, name="idle", align_bytes=TURNED)
        nc.vector.memset(idle[:], 0.0)
        idle_turned = held.tile([P, SQUARE], F32, name="idle_turned", align_bytes=TURNED)
        nc.vector.transpose(idle_turned[:], idle[:])
        idle_repeated = held.tile([P, CHUNKS, SQUARE], F32, name="idle_repeated")
        nc.vector.tensor_copy(idle_repeated[:], idle_turned[:, 0:CHUNKS].unsqueeze(2).to_broadcast([P, CHUNKS, SQUARE]))
        idle_product = held.tile([P, SQUARE], F32, name="idle_product")
        nc.vector.tensor_tensor(idle_product[:], idle[:], idle_turned[:], mybir.AluOpType.mult)

        columns = held.tile([P, SQUARE], F32, name="columns", align_bytes=BLOCK)
        nc.vector.transpose(columns[:], chunks[:])
        repeated = held.tile([P, CHUNKS, SQUARE], F32, name="repeated", align_bytes=RUN)
        factor = held.tile([P, N], F32, name="factor", align_bytes=RUN)
        for e in range(E):
            own = slice(e * CHUNKS // E, (e + 1) * CHUNKS // E)
            nc.vector.tensor_copy(repeated[:, own, :], columns[:, own].unsqueeze(2).to_broadcast([P, CHUNKS // E, SQUARE]))
        for e in range(E):
            own = slice(e * CHUNKS // E, (e + 1) * CHUNKS // E)
            nc.vector.transpose(factor[:, e * Q : (e + 1) * Q], repeated[:, own, :].rearrange("p b i -> p (b i)"))

        result = held.tile([P, N], F32, name="result", align_bytes=RUN)
        for e in range(E):
            piece = offsets[:, e * Q // PER_COLUMN : (e + 1) * Q // PER_COLUMN]
            entries = slice(e * Q, (e + 1) * Q)
            bank = psum.tile([P, Q], F32, name="bank%d" % e)
            for b in range(KB):
                nc.tensor.matmul(
                    bank[:],
                    weights[e][:, b * M : (b + 1) * M],
                    windows[b][:].indirect(piece),
                    start=(b == 0),
                    stop=(b == KB - 1),
                )
            nc.vector.tensor_tensor(result[:, entries], bank[:], factor[:, entries], mybir.AluOpType.mult)
            nc.sync.dma_start(out[:, entries], result[:, entries])

        kept_busy = [held.tile([P, SQUARE], F32, name="kept_busy%d" % step) for step in range(BUSY_STEPS)]
        nc.vector.tensor_copy(kept_busy[0][:], result[:, N - SQUARE : N])
        for step in range(1, BUSY_STEPS):
            nc.vector.tensor_copy(kept_busy[step][:], kept_busy[step - 1][:])
